import numpy as np
import ml_dtypes


def mxq(x, axis, fmt="e4m3"):
    dtype, down = {"e4m3": (ml_dtypes.float8_e4m3fn, 7), "e5m2": (ml_dtypes.float8_e5m2, 14)}[fmt]
    v = np.moveaxis(np.asarray(x, np.float32).astype(ml_dtypes.bfloat16).astype(np.float64), axis, -1)
    blocks = v.reshape(v.shape[:-1] + (-1, 32))
    amax = np.abs(blocks).max(-1, keepdims=True)
    byte = np.maximum(np.where(amax > 0, np.frexp(amax)[1] - 1 + 127, 0) - down, 1)
    scale = np.exp2(byte - 127.0)
    codes = (blocks / scale).astype(np.float32).astype(dtype).astype(np.float64)
    return np.moveaxis((codes * scale).reshape(v.shape), -1, axis)


WIDE = False


def mx_kscale(k):
    if not WIDE:
        return np.ones(k)
    levels = np.array([10, -10, 5, -5, 0])
    if k % 512:
        return np.exp2(np.random.permutation(np.resize(levels, k // 32))).repeat(32)
    a = np.empty((k // 512, 16))
    for p in range(k // 512):
        a[p, :8] = np.random.permutation(np.resize(levels, 8))
        for g in range(8):
            far = levels[np.abs(levels - a[p, g]) >= 10]
            a[p, g + 8] = far[np.random.randint(len(far))]
    return np.exp2(a.ravel()).repeat(32)


def f64(x):
    return np.asarray(x).astype(np.float64)


def striped(idx):
    return np.tile(np.asarray(idx).reshape(-1, 16).T, (8, 1)).astype(np.uint16)


def unstriped(offs):
    return offs[:16].T.reshape(-1).astype(np.int64)


E2M1 = np.array([0.0, 0.5, 1.0, 1.5, 2.0, 3.0, 4.0, 6.0, -0.0, -0.5, -1.0, -1.5, -2.0, -3.0, -4.0, -6.0])


def pack_weight(w, fmt):
    k, n = w.shape
    w = f64(np.asarray(w, np.float32).astype(ml_dtypes.bfloat16)).reshape(k // 32, 32, n)
    amax = np.abs(w).max(1)
    if fmt == "e4m3":
        byte = np.frexp(amax)[1] - 1 + 127 - 7
    else:
        mant, ex = np.frexp(amax / 6.0)
        byte = np.where(mant > 0.5, ex, ex - 1) + 127
    byte = np.clip(np.where(amax > 0, byte, 1), 1, 254)
    scaled = (w * np.exp2(127.0 - byte)[:, None, :]).reshape(k, n).astype(np.float32)
    by_word = np.ascontiguousarray(scaled.reshape(k // 512, 128, 4, n).transpose(0, 1, 3, 2))
    if fmt == "e4m3":
        words = by_word.astype(ml_dtypes.float8_e4m3fn).view(np.uint8)
    else:
        c = by_word.astype(ml_dtypes.float4_e2m1fn).view(np.uint8) & 0xF
        words = (c[..., 0::2] | (c[..., 1::2] << 4)).reshape(k // 512, 128, 2 * n)
    return np.ascontiguousarray(words), np.ascontiguousarray(byte.astype(np.uint8).reshape(k // 512, 16, n))


def unpack_weight(words, scales, fmt):
    g, _, n = scales.shape
    words = np.ascontiguousarray(words).reshape(g, 128, n, -1)
    if fmt == "e4m3":
        vals = words.view(ml_dtypes.float8_e4m3fn).astype(np.float64)
    else:
        nib = np.empty((g, 128, n, 4), np.uint8)
        nib[..., 0::2] = words & 0xF
        nib[..., 1::2] = words >> 4
        vals = E2M1[nib]
    vals = vals * np.repeat(np.exp2(scales.astype(np.float64) - 127.0), 8, axis=1)[..., None]
    return vals.transpose(0, 1, 3, 2).reshape(g * 512, n)


D, E, T, I, Q = 512, 512, 2048, 512, 128


def setup_inputs():
    n = np.random.standard_normal
    idx = np.random.permutation(T)[:I]
    fd = mx_kscale(D)
    fe = mx_kscale(E)
    keysp = pack_weight(n((D, T)) / fd[:, None], "e4m3")
    valsp = pack_weight(n((E, T)) / fe[:, None], "e4m3")
    return {
        "query": (n((D, Q)) * 1.0 / np.sqrt(D) * fd[:, None]).astype(np.float32),
        "keys_words": keysp[0],
        "keys_scales": keysp[1],
        "sharp": (np.random.uniform(0.4, 1.0, (Q, 1))).astype(np.float32),
        "gout": (n((E, Q)) * 1 / np.sqrt(E) * fe[:, None]).astype(np.float32),
        "vals_words": valsp[0],
        "vals_scales": valsp[1],
        "old": (0.5 * n((Q, T))).astype(np.float32),
        "offs": striped(idx),
    }


def reference(query, keys_words, keys_scales, sharp, gout, vals_words, vals_scales, old, offs):
    idx = unstriped(offs)
    keysu = unpack_weight(keys_words, keys_scales, "e4m3")
    valsu = unpack_weight(vals_words, vals_scales, "e4m3")
    queryq = mxq(f64(query), 0, "e4m3")
    keysidxg = keysu[:, idx]
    a = queryq.T @ keysidxg
    m1 = np.mean(a, axis=1, keepdims=True)
    ce = a - m1
    sd = np.sqrt(np.mean(np.square(ce), axis=1, keepdims=True) + 0.05)
    s = ce / sd * f64(sharp)
    p = np.exp(s - np.max(s, axis=1, keepdims=True))
    z = np.sum(p, axis=1, keepdims=True)
    goutq = mxq(f64(gout), 0, "e4m3")
    valsidxg = valsu[:, idx]
    c0 = goutq.T @ valsidxg
    dz = np.sum(c0 * p / np.square(z) * (-1.0), axis=1, keepdims=True)
    dp = c0 / z + dz
    ds = dp * p
    dsd = np.sum(ds * f64(sharp) * ce / np.square(sd) * (-1.0), axis=1, keepdims=True)
    dce = ds * f64(sharp) / sd + dsd * 0.5 / np.sqrt(np.mean(np.square(ce), axis=1, keepdims=True) + 0.05) / 512.0 * ce * 2.0
    dm1 = np.sum(dce * (-1.0), axis=1, keepdims=True)
    da = dce + dm1 / 512.0
    gs = da * 512.0
    gf = np.zeros((Q, T))
    gf[:, idx] = gs
    y = f64(old) + gf
    return y

@@ -1,0 +1,146 @@
+from contextlib import ExitStack
+
+import concourse.mybir as mybir
+
+D, E, T, I, Q = 512, 512, 2048, 512, 128
+FLOPS = 2 * D * Q * I + 2 * E * Q * I
+
+F32 = mybir.dt.float32
+BF16 = mybir.dt.bfloat16
+I32 = mybir.dt.int32
+U32 = mybir.dt.uint32
+U16 = mybir.dt.uint16
+U8 = mybir.dt.uint8
+FP8X4 = mybir.dt.float8_e4m3fn_x4
+ALU = mybir.AluOpType
+ACT = mybir.ActivationFunctionType
+
+P = 128
+PACK = 4
+EPS = 0.05
+VALS_PLANE = 4
+STORE_COLS = [512, 512, 512, 512]
+
+
+def load_scale_rows(queue, plane, scales, first):
+    for quad in range(4):
+        queue.dma_start(
+            out=plane[32 * quad + first : 32 * quad + first + 4, :].bitcast(I32),
+            in_=scales[0, 4 * quad : 4 * quad + 4, :].bitcast(I32),
+        )
+
+
+def load_words(queue, tile, words):
+    queue.dma_start(out=tile[:].bitcast(I32), in_=words[0].rearrange("p n t -> p (n t)").bitcast(I32))
+
+
+def tile_attend_bstandardised_s_kernel(tc, query, keys_words, keys_scales, sharp, gout, vals_words, vals_scales, old, offs, out):
+    nc = tc.nc
+    with ExitStack() as ctx:
+        sb = ctx.enter_context(tc.tile_pool(name="sb", bufs=1))
+        ps = ctx.enter_context(tc.psum_pool(name="ps", bufs=1))
+
+        offsets = sb.tile([P, I // 16], U16, name="offsets")
+        q_raw = sb.tile([P, PACK, Q], F32, name="q_raw", tag="q_then_v", align_bytes=64)
+        g_raw = sb.tile([P, PACK, Q], F32, name="g_raw", tag="g_then_old")
+        k_pool = sb.tile([P, T], U32, name="k_pool", align_bytes=64)
+        ks_pool = sb.tile([P, T], U8, name="ks_pool", tag="ks_then_placed", align_bytes=64)
+        vs_pool = sb.tile([P, T], U8, name="vs_pool", align_bytes=64)
+        pair = sb.tile([P, 2], F32, name="pair")
+        neg_sharp = sb.tile([P, 1], F32, name="neg_sharp")
+        minus_half = sb.tile([P, 1], F32, name="minus_half")
+
+        nc.vector.memset(ks_pool[:].bitcast(I32), 0)
+        nc.gpsimd.dma_start(out=pair[:, 0:1], in_=sharp)
+        nc.gpsimd.memset(vs_pool[:].bitcast(I32), 0)
+        load_scale_rows(nc.gpsimd, vs_pool, vals_scales, VALS_PLANE)
+        nc.gpsimd.memset(minus_half[:], -0.5)
+        nc.gpsimd.tensor_scalar(neg_sharp[:], pair[:, 0:1], -1.0, 1.0, ALU.mult, ALU.mult)
+
+        nc.sync.dma_start(offsets[:], offs)
+        nc.sync.dma_start(out=q_raw[:], in_=query.rearrange("(p j) w -> p j w", j=PACK))
+        load_scale_rows(nc.scalar, ks_pool, keys_scales, 0)
+        load_words(nc.sync, k_pool, keys_words)
+        nc.sync.dma_start(out=g_raw[:], in_=gout.rearrange("(p j) w -> p j w", j=PACK))
+
+        def quantise(grouped, name):
+            codes = sb.tile([P, Q], U32, name=name + "_codes", align_bytes=64)
+            plane = sb.tile([P, Q], U8, name=name + "_plane", align_bytes=64)
+            nc.vector.quantize_mx(out=codes[:].bitcast(FP8X4), scales=plane[:], in_=grouped[:].rearrange("p w j -> p (w j)"))
+            return codes, plane
+
+        def gather(pool_tile, dtype, name):
+            picked = sb.tile([P, I], dtype, name=name, align_bytes=64)
+            nc.vector.tensor_copy(picked[:], pool_tile[:].indirect(offsets[:]))
+            return picked
+
+        q_grouped = sb.tile([P, Q, PACK], BF16, name="q_grouped", align_bytes=64)
+        nc.scalar.copy(out=q_grouped[:], in_=q_raw[:].rearrange("p j w -> p w j"))
+        v_pool = sb.tile([P, T], U32, name="v_pool", tag="q_then_v", align_bytes=64)
+        load_words(nc.sync, v_pool, vals_words)
+        g_grouped = sb.tile([P, Q, PACK], BF16, name="g_grouped", align_bytes=64)
+        nc.scalar.activation(out=g_grouped[:], in_=g_raw[:].rearrange("p j w -> p w j"), func=ACT.Copy)
+        old_sb = sb.tile([P, T], F32, name="old_sb", tag="g_then_old")
+        nc.sync.dma_start(out=old_sb[:], in_=old)
+        ks = gather(ks_pool, U8, "ks")
+        q_codes, q_plane = quantise(q_grouped, "q")
+        placed = sb.tile([P, T], F32, name="placed", tag="ks_then_placed", align_bytes=64)
+        nc.vector.memset(placed[:], 0.0)
+        kw = gather(k_pool, U32, "kw")
+        a = ps.tile([P, I], F32, name="a")
+        nc.tensor.matmul_mx(out=a[:], lhsT=q_codes[:].bitcast(FP8X4), lhsT_scale=q_plane[:], rhs=kw[:].bitcast(FP8X4), rhs_scale=ks[:], start=True, stop=True)
+        vs = gather(vs_pool, U8, "vs")
+        g_codes, g_plane = quantise(g_grouped, "g")
+
+        stats = sb.tile([P, 6], F32, name="stats")
+        mean_var = sb.tile([P, 2], F32, name="mean_var")
+        nc.vector.bn_stats(stats[:], a[:])
+        nc.vector.bn_aggr(mean_var[:], stats[:])
+        spread2 = sb.tile([P, 1], F32, name="spread2")
+        inv_sd = sb.tile([P, 1], F32, name="inv_sd")
+        nc.gpsimd.tensor_scalar(spread2[:], mean_var[:, 1:2], EPS, 1.0, ALU.add, ALU.mult)
+        nc.gpsimd.tensor_tensor(inv_sd[:], spread2[:], minus_half[:], ALU.pow)
+        signed = sb.tile([P, I], F32, name="signed")
+        nc.vector.tensor_scalar(signed[:], a[:], neg_sharp[:], None, ALU.mult, ALU.min, accum_out=pair[:, 1:2])
+
+        vw = gather(v_pool, U32, "vw")
+        c0 = ps.tile([P, I], F32, name="c0")
+        nc.tensor.matmul_mx(out=c0[:], lhsT=g_codes[:].bitcast(FP8X4), lhsT_scale=g_plane[:], rhs=vw[:].bitcast(FP8X4), rhs_scale=vs[VALS_PLANE:P, :], start=True, stop=True)
+
+        slope_shift = sb.tile([P, 2], F32, name="slope_shift")
+        nc.scalar.activation(out=slope_shift[:], in_=pair[:], func=ACT.Copy, scale=inv_sd[:])
+        p = sb.tile([P, I], F32, name="p")
+        z = sb.tile([P, 1], F32, name="z")
+        nc.scalar.activation(out=p[:], in_=a[:], func=ACT.Exp, scale=slope_shift[:, 0:1], bias=slope_shift[:, 1:2], accum_out=z[:])
+        neg_ce = sb.tile([P, I], F32, name="neg_ce")
+        nc.scalar.activation(out=neg_ce[:], in_=a[:], func=ACT.Identity, scale=-1.0, bias=mean_var[:, 0:1])
+        inv_var = sb.tile([P, 1], F32, name="inv_var")
+        nc.scalar.activation(out=inv_var[:], in_=inv_sd[:], func=ACT.Square)
+
+        inv_z = sb.tile([P, 1], F32, name="inv_z", tag="q_then_v", align_bytes=64)
+        gain = sb.tile([P, 1], F32, name="gain")
+        nc.vector.reciprocal(inv_z[:], z[:])
+        nc.vector.tensor_scalar(gain[:], inv_z[:], slope_shift[:, 0:1], -float(I), ALU.mult, ALU.mult)
+        w = sb.tile([P, I], F32, name="w")
+        nc.scalar.activation(out=w[:], in_=p[:], func=ACT.Copy, scale=inv_z[:])
+
+        pc = sb.tile([P, I], F32, name="pc")
+        pc_sum = sb.tile([P, 1], F32, name="pc_sum")
+        nc.vector.scalar_tensor_tensor(pc[:], c0[:], gain[:], p[:], ALU.mult, ALU.mult, accum_out=pc_sum[:])
+        direct = sb.tile([P, I], F32, name="direct")
+        nc.vector.scalar_tensor_tensor(direct[:], w[:], pc_sum[:], pc[:], ALU.mult, ALU.subtract)
+        terms = sb.tile([P, I], F32, name="terms")
+        through_sd = sb.tile([P, 1], F32, name="through_sd")
+        nc.vector.scalar_tensor_tensor(terms[:], direct[:], inv_var[:], neg_ce[:], ALU.mult, ALU.mult, accum_out=through_sd[:])
+        indirect_part = sb.tile([P, I], F32, name="indirect_part")
+        nc.vector.tensor_scalar(indirect_part[:], neg_ce[:], through_sd[:], -1.0 / I, ALU.mult, ALU.mult)
+        nc.vector.tensor_tensor(placed[:].indirect(offsets[:]), direct[:], indirect_part[:], ALU.add)
+
+        start = 0
+        for n, width in enumerate(STORE_COLS):
+            cols = slice(start, start + width)
+            total = sb.tile([P, width], F32, name="total%d" % n)
+            nc.vector.tensor_tensor(total[:], placed[:, cols], old_sb[:, cols], ALU.add)
+            queue = nc.sync if n % 2 == 0 else nc.scalar
+            queue.dma_start(out=out[:, cols], in_=total[:])
+            start = start + width

@@ -19,7 +19,7 @@ P = 128
 PACK = 4
 EPS = 0.05
 VALS_PLANE = 4
-STORE_COLS = [512, 512, 512, 512]
+STORE_COLS = [256, 384, 384, 384, 384, 256]
 
 
 def load_scale_rows(queue, plane, scales, first):
@@ -38,86 +38,96 @@ def tile_attend_bstandardised_s_kernel(tc, query, keys_words, keys_scales, sharp
     nc = tc.nc
     with ExitStack() as ctx:
         sb = ctx.enter_context(tc.tile_pool(name="sb", bufs=1))
+        shared = ctx.enter_context(tc.tile_pool(name="shared", bufs=1))
         ps = ctx.enter_context(tc.psum_pool(name="ps", bufs=1))
 
         offsets = sb.tile([P, I // 16], U16, name="offsets")
-        q_raw = sb.tile([P, PACK, Q], F32, name="q_raw", tag="q_then_v", align_bytes=64)
-        g_raw = sb.tile([P, PACK, Q], F32, name="g_raw", tag="g_then_old")
-        k_pool = sb.tile([P, T], U32, name="k_pool", align_bytes=64)
-        ks_pool = sb.tile([P, T], U8, name="ks_pool", tag="ks_then_placed", align_bytes=64)
+        q_raw = sb.tile([P, PACK, Q], F32, name="q_raw")
+        g_raw = shared.tile([P, PACK, Q], F32, name="g_raw", align_bytes=64, offset=9 * T)
+        k_pool = shared.tile([P, T], U32, name="k_pool", align_bytes=64, offset=0)
+        v_pool = shared.tile([P, T], U32, name="v_pool", align_bytes=64, offset=4 * T)
+        ks_pool = sb.tile([P, T], U8, name="ks_pool", align_bytes=64)
         vs_pool = sb.tile([P, T], U8, name="vs_pool", align_bytes=64)
+        old_sb = sb.tile([P, T], F32, name="old_sb")
+        placed = sb.tile([P, T], F32, name="placed")
         pair = sb.tile([P, 2], F32, name="pair")
         neg_sharp = sb.tile([P, 1], F32, name="neg_sharp")
         minus_half = sb.tile([P, 1], F32, name="minus_half")
 
-        nc.vector.memset(ks_pool[:].bitcast(I32), 0)
+        nc.vector.memset(ks_pool[:, 0 : T // 2].bitcast(I32), 0)
+        nc.gpsimd.memset(ks_pool[:, T // 2 : T].bitcast(I32), 0)
         nc.gpsimd.dma_start(out=pair[:, 0:1], in_=sharp)
-        nc.gpsimd.memset(vs_pool[:].bitcast(I32), 0)
-        load_scale_rows(nc.gpsimd, vs_pool, vals_scales, VALS_PLANE)
+        nc.vector.memset(vs_pool[:].bitcast(I32), 0)
+        nc.vector.memset(placed[:], 0.0)
         nc.gpsimd.memset(minus_half[:], -0.5)
-        nc.gpsimd.tensor_scalar(neg_sharp[:], pair[:, 0:1], -1.0, 1.0, ALU.mult, ALU.mult)
 
         nc.sync.dma_start(offsets[:], offs)
         nc.sync.dma_start(out=q_raw[:], in_=query.rearrange("(p j) w -> p j w", j=PACK))
-        load_scale_rows(nc.scalar, ks_pool, keys_scales, 0)
+        load_scale_rows(nc.sync, ks_pool, keys_scales, 0)
         load_words(nc.sync, k_pool, keys_words)
+        load_scale_rows(nc.sync, vs_pool, vals_scales, VALS_PLANE)
         nc.sync.dma_start(out=g_raw[:], in_=gout.rearrange("(p j) w -> p j w", j=PACK))
+        load_words(nc.sync, v_pool, vals_words)
+        nc.sync.dma_start(out=old_sb[:], in_=old)
 
-        def quantise(grouped, name):
-            codes = sb.tile([P, Q], U32, name=name + "_codes", align_bytes=64)
+        def round_and_interleave(raw, name):
+            grouped = sb.tile([P, Q, PACK], BF16, name=name, align_bytes=64)
+            nc.scalar.activation(out=grouped[:], in_=raw[:].rearrange("p j w -> p w j"), func=ACT.Copy)
+            return grouped
+
+        def quantise(grouped, codes, name):
             plane = sb.tile([P, Q], U8, name=name + "_plane", align_bytes=64)
             nc.vector.quantize_mx(out=codes[:].bitcast(FP8X4), scales=plane[:], in_=grouped[:].rearrange("p w j -> p (w j)"))
-            return codes, plane
+            return plane
 
-        def gather(pool_tile, dtype, name):
-            picked = sb.tile([P, I], dtype, name=name, align_bytes=64)
+        def gather(picked, pool_tile):
             nc.vector.tensor_copy(picked[:], pool_tile[:].indirect(offsets[:]))
-            return picked
 
-        q_grouped = sb.tile([P, Q, PACK], BF16, name="q_grouped", align_bytes=64)
-        nc.scalar.copy(out=q_grouped[:], in_=q_raw[:].rearrange("p j w -> p w j"))
-        v_pool = sb.tile([P, T], U32, name="v_pool", tag="q_then_v", align_bytes=64)
-        load_words(nc.sync, v_pool, vals_words)
-        g_grouped = sb.tile([P, Q, PACK], BF16, name="g_grouped", align_bytes=64)
-        nc.scalar.activation(out=g_grouped[:], in_=g_raw[:].rearrange("p j w -> p w j"), func=ACT.Copy)
-        old_sb = sb.tile([P, T], F32, name="old_sb", tag="g_then_old")
-        nc.sync.dma_start(out=old_sb[:], in_=old)
-        ks = gather(ks_pool, U8, "ks")
-        q_codes, q_plane = quantise(q_grouped, "q")
-        placed = sb.tile([P, T], F32, name="placed", tag="ks_then_placed", align_bytes=64)
-        nc.vector.memset(placed[:], 0.0)
-        kw = gather(k_pool, U32, "kw")
+        q_grouped = round_and_interleave(q_raw, "q_grouped")
+        g_grouped = round_and_interleave(g_raw, "g_grouped")
+        ks = sb.tile([P, I], U8, name="ks", align_bytes=64)
+        gather(ks, ks_pool)
+        q_codes = sb.tile([P, Q], U32, name="q_codes", align_bytes=64)
+        q_plane = quantise(q_grouped, q_codes, "q")
+        nc.gpsimd.tensor_scalar(neg_sharp[:], pair[:, 0:1], -1.0, 1.0, ALU.mult, ALU.mult)
+        kw = sb.tile([P, I], U32, name="kw", align_bytes=64)
+        gather(kw, k_pool)
         a = ps.tile([P, I], F32, name="a")
         nc.tensor.matmul_mx(out=a[:], lhsT=q_codes[:].bitcast(FP8X4), lhsT_scale=q_plane[:], rhs=kw[:].bitcast(FP8X4), rhs_scale=ks[:], start=True, stop=True)
-        vs = gather(vs_pool, U8, "vs")
-        g_codes, g_plane = quantise(g_grouped, "g")
+        vs = shared.tile([P, I], U8, name="vs", align_bytes=64, offset=0)
+        gather(vs, vs_pool)
 
-        stats = sb.tile([P, 6], F32, name="stats")
+        stats = shared.tile([P, 6], F32, name="stats", align_bytes=64, offset=8 * T)
         mean_var = sb.tile([P, 2], F32, name="mean_var")
         nc.vector.bn_stats(stats[:], a[:])
         nc.vector.bn_aggr(mean_var[:], stats[:])
         spread2 = sb.tile([P, 1], F32, name="spread2")
         inv_sd = sb.tile([P, 1], F32, name="inv_sd")
-        nc.gpsimd.tensor_scalar(spread2[:], mean_var[:, 1:2], EPS, 1.0, ALU.add, ALU.mult)
+        nc.vector.tensor_scalar(spread2[:], mean_var[:, 1:2], EPS, None, ALU.add)
         nc.gpsimd.tensor_tensor(inv_sd[:], spread2[:], minus_half[:], ALU.pow)
+        inv_var = sb.tile([P, 1], F32, name="inv_var")
+        nc.gpsimd.tensor_tensor(inv_var[:], inv_sd[:], inv_sd[:], ALU.mult)
         signed = sb.tile([P, I], F32, name="signed")
         nc.vector.tensor_scalar(signed[:], a[:], neg_sharp[:], None, ALU.mult, ALU.min, accum_out=pair[:, 1:2])
 
-        vw = gather(v_pool, U32, "vw")
+        g_codes = shared.tile([P, Q], U32, name="g_codes", align_bytes=64, offset=8 * T)
+        g_plane = quantise(g_grouped, g_codes, "g")
+        vw = sb.tile([P, I], U32, name="vw", align_bytes=64)
         c0 = ps.tile([P, I], F32, name="c0")
-        nc.tensor.matmul_mx(out=c0[:], lhsT=g_codes[:].bitcast(FP8X4), lhsT_scale=g_plane[:], rhs=vw[:].bitcast(FP8X4), rhs_scale=vs[VALS_PLANE:P, :], start=True, stop=True)
+        for half in range(2):
+            slots = slice(half * I // 2, (half + 1) * I // 2)
+            nc.vector.tensor_copy(vw[:, slots], v_pool[:].indirect(offsets[:, half * I // 32 : (half + 1) * I // 32]))
+            nc.tensor.matmul_mx(out=c0[:, slots], lhsT=g_codes[:].bitcast(FP8X4), lhsT_scale=g_plane[:], rhs=vw[:, slots].bitcast(FP8X4), rhs_scale=vs[VALS_PLANE:P, slots], start=True, stop=True)
 
-        slope_shift = sb.tile([P, 2], F32, name="slope_shift")
+        slope_shift = shared.tile([P, 2], F32, name="slope_shift", align_bytes=64, offset=9 * T)
         nc.scalar.activation(out=slope_shift[:], in_=pair[:], func=ACT.Copy, scale=inv_sd[:])
         p = sb.tile([P, I], F32, name="p")
         z = sb.tile([P, 1], F32, name="z")
         nc.scalar.activation(out=p[:], in_=a[:], func=ACT.Exp, scale=slope_shift[:, 0:1], bias=slope_shift[:, 1:2], accum_out=z[:])
         neg_ce = sb.tile([P, I], F32, name="neg_ce")
         nc.scalar.activation(out=neg_ce[:], in_=a[:], func=ACT.Identity, scale=-1.0, bias=mean_var[:, 0:1])
-        inv_var = sb.tile([P, 1], F32, name="inv_var")
-        nc.scalar.activation(out=inv_var[:], in_=inv_sd[:], func=ACT.Square)
 
-        inv_z = sb.tile([P, 1], F32, name="inv_z", tag="q_then_v", align_bytes=64)
+        inv_z = shared.tile([P, 1], F32, name="inv_z", align_bytes=64, offset=4 * T)
         gain = sb.tile([P, 1], F32, name="gain")
         nc.vector.reciprocal(inv_z[:], z[:])
         nc.vector.tensor_scalar(gain[:], inv_z[:], slope_shift[:, 0:1], -float(I), ALU.mult, ALU.mult)

@@ -23,10 +23,10 @@ STORE_COLS = [256, 384, 384, 384, 384, 256]
 
 
 def load_scale_rows(queue, plane, scales, first):
-    for quad in range(4):
+    for row in range(4):
         queue.dma_start(
-            out=plane[32 * quad + first : 32 * quad + first + 4, :].bitcast(I32),
-            in_=scales[0, 4 * quad : 4 * quad + 4, :].bitcast(I32),
+            out=plane[first + row : P : 32, :].bitcast(I32),
+            in_=scales[0, row:16:4, :].bitcast(I32),
         )
 
 
@@ -50,13 +50,14 @@ def tile_attend_bstandardised_s_kernel(tc, query, keys_words, keys_scales, sharp
         vs_pool = sb.tile([P, T], U8, name="vs_pool", align_bytes=64)
         old_sb = sb.tile([P, T], F32, name="old_sb")
         placed = sb.tile([P, T], F32, name="placed")
-        pair = sb.tile([P, 2], F32, name="pair")
-        neg_sharp = sb.tile([P, 1], F32, name="neg_sharp")
+        sharp_sb = sb.tile([P, 1], F32, name="sharp_sb")
+        sharp_up = sb.tile([P, 1], F32, name="sharp_up")
+        sharp_down = sb.tile([P, 1], F32, name="sharp_down")
         minus_half = sb.tile([P, 1], F32, name="minus_half")
 
         nc.vector.memset(ks_pool[:, 0 : T // 2].bitcast(I32), 0)
         nc.gpsimd.memset(ks_pool[:, T // 2 : T].bitcast(I32), 0)
-        nc.gpsimd.dma_start(out=pair[:, 0:1], in_=sharp)
+        nc.gpsimd.dma_start(out=sharp_sb[:], in_=sharp)
         nc.vector.memset(vs_pool[:].bitcast(I32), 0)
         nc.vector.memset(placed[:], 0.0)
         nc.gpsimd.memset(minus_half[:], -0.5)
@@ -84,34 +85,45 @@ def tile_attend_bstandardised_s_kernel(tc, query, keys_words, keys_scales, sharp
             nc.vector.tensor_copy(picked[:], pool_tile[:].indirect(offsets[:]))
 
         q_grouped = round_and_interleave(q_raw, "q_grouped")
+        nc.gpsimd.tensor_scalar(sharp_up[:], sharp_sb[:], float(I), 1.0, ALU.mult, ALU.mult)
+        nc.gpsimd.tensor_scalar(sharp_down[:], sharp_sb[:], -float(I), 1.0, ALU.mult, ALU.mult)
         g_grouped = round_and_interleave(g_raw, "g_grouped")
         ks = sb.tile([P, I], U8, name="ks", align_bytes=64)
         gather(ks, ks_pool)
         q_codes = sb.tile([P, Q], U32, name="q_codes", align_bytes=64)
         q_plane = quantise(q_grouped, q_codes, "q")
-        nc.gpsimd.tensor_scalar(neg_sharp[:], pair[:, 0:1], -1.0, 1.0, ALU.mult, ALU.mult)
         kw = sb.tile([P, I], U32, name="kw", align_bytes=64)
-        gather(kw, k_pool)
-        a = ps.tile([P, I], F32, name="a")
-        nc.tensor.matmul_mx(out=a[:], lhsT=q_codes[:].bitcast(FP8X4), lhsT_scale=q_plane[:], rhs=kw[:].bitcast(FP8X4), rhs_scale=ks[:], start=True, stop=True)
+        a = [ps.tile([P, I // 2], F32, name="a%d" % half) for half in range(2)]
+        for half in range(2):
+            slots = slice(half * I // 2, (half + 1) * I // 2)
+            nc.vector.tensor_copy(kw[:, slots], k_pool[:].indirect(offsets[:, half * I // 32 : (half + 1) * I // 32]))
+            nc.tensor.matmul_mx(out=a[half][:], lhsT=q_codes[:].bitcast(FP8X4), lhsT_scale=q_plane[:], rhs=kw[:, slots].bitcast(FP8X4), rhs_scale=ks[:, slots], start=True, stop=True)
         vs = shared.tile([P, I], U8, name="vs", align_bytes=64, offset=0)
         gather(vs, vs_pool)
 
-        stats = shared.tile([P, 6], F32, name="stats", align_bytes=64, offset=8 * T)
-        mean_var = sb.tile([P, 2], F32, name="mean_var")
-        nc.vector.bn_stats(stats[:], a[:])
-        nc.vector.bn_aggr(mean_var[:], stats[:])
+        g_codes = shared.tile([P, Q], U32, name="g_codes", align_bytes=64, offset=T)
+        g_plane = quantise(g_grouped, g_codes, "g")
+
+        scores = shared.tile([P, I], F32, name="scores", align_bytes=64, offset=9 * T)
+        half_means = sb.tile([P, 2], F32, name="half_means")
+        neg_mean = sb.tile([P, 1], F32, name="neg_mean")
+        squares = sb.tile([P, I], F32, name="squares")
+        square_sum = shared.tile([P, 1], F32, name="square_sum", align_bytes=64, offset=8 * T)
         spread2 = sb.tile([P, 1], F32, name="spread2")
         inv_sd = sb.tile([P, 1], F32, name="inv_sd")
-        nc.vector.tensor_scalar(spread2[:], mean_var[:, 1:2], EPS, None, ALU.add)
+        for half in range(2):
+            slots = slice(half * I // 2, (half + 1) * I // 2)
+            nc.scalar.activation(out=scores[:, slots], in_=a[half][:], func=ACT.Copy, scale=-1.0 / I, accum_out=half_means[:, half : half + 1])
+        nc.scalar.activation(out=neg_mean[:], in_=half_means[:, 0:1], func=ACT.Identity, bias=half_means[:, 1:2])
+        nc.scalar.activation(out=squares[:], in_=scores[:], func=ACT.Square, scale=-float(I), bias=neg_mean[:], accum_out=square_sum[:])
+        nc.scalar.activation(out=spread2[:], in_=square_sum[:], func=ACT.Copy, scale=1.0 / I, bias=EPS)
         nc.gpsimd.tensor_tensor(inv_sd[:], spread2[:], minus_half[:], ALU.pow)
-        inv_var = sb.tile([P, 1], F32, name="inv_var")
-        nc.gpsimd.tensor_tensor(inv_var[:], inv_sd[:], inv_sd[:], ALU.mult)
         signed = sb.tile([P, I], F32, name="signed")
-        nc.vector.tensor_scalar(signed[:], a[:], neg_sharp[:], None, ALU.mult, ALU.min, accum_out=pair[:, 1:2])
+        neg_top = sb.tile([P, 1], F32, name="neg_top")
+        nc.vector.tensor_scalar(signed[:], scores[:], sharp_up[:], None, ALU.mult, ALU.min, accum_out=neg_top[:])
+        below_top = shared.tile([P, I], F32, name="below_top", align_bytes=64, offset=8 * T)
+        nc.scalar.activation(out=below_top[:], in_=signed[:], func=ACT.Identity, scale=-1.0, bias=neg_top[:])
 
-        g_codes = shared.tile([P, Q], U32, name="g_codes", align_bytes=64, offset=8 * T)
-        g_plane = quantise(g_grouped, g_codes, "g")
         vw = sb.tile([P, I], U32, name="vw", align_bytes=64)
         c0 = ps.tile([P, I], F32, name="c0")
         for half in range(2):
@@ -119,31 +131,33 @@ def tile_attend_bstandardised_s_kernel(tc, query, keys_words, keys_scales, sharp
             nc.vector.tensor_copy(vw[:, slots], v_pool[:].indirect(offsets[:, half * I // 32 : (half + 1) * I // 32]))
             nc.tensor.matmul_mx(out=c0[:, slots], lhsT=g_codes[:].bitcast(FP8X4), lhsT_scale=g_plane[:], rhs=vw[:, slots].bitcast(FP8X4), rhs_scale=vs[VALS_PLANE:P, slots], start=True, stop=True)
 
-        slope_shift = shared.tile([P, 2], F32, name="slope_shift", align_bytes=64, offset=9 * T)
-        nc.scalar.activation(out=slope_shift[:], in_=pair[:], func=ACT.Copy, scale=inv_sd[:])
+        ce = shared.tile([P, I], F32, name="ce", align_bytes=64, offset=5 * T)
+        nc.vector.tensor_scalar(ce[:], scores[:], -float(I), neg_mean[:], ALU.mult, ALU.add)
+        gain = shared.tile([P, 1], F32, name="gain", align_bytes=64, offset=6 * T)
+        nc.vector.tensor_tensor(gain[:], sharp_down[:], inv_sd[:], ALU.mult)
         p = sb.tile([P, I], F32, name="p")
         z = sb.tile([P, 1], F32, name="z")
-        nc.scalar.activation(out=p[:], in_=a[:], func=ACT.Exp, scale=slope_shift[:, 0:1], bias=slope_shift[:, 1:2], accum_out=z[:])
-        neg_ce = sb.tile([P, I], F32, name="neg_ce")
-        nc.scalar.activation(out=neg_ce[:], in_=a[:], func=ACT.Identity, scale=-1.0, bias=mean_var[:, 0:1])
+        nc.scalar.activation(out=p[:], in_=below_top[:], func=ACT.Exp, scale=inv_sd[:], accum_out=z[:])
 
         inv_z = shared.tile([P, 1], F32, name="inv_z", align_bytes=64, offset=4 * T)
-        gain = sb.tile([P, 1], F32, name="gain")
         nc.vector.reciprocal(inv_z[:], z[:])
-        nc.vector.tensor_scalar(gain[:], inv_z[:], slope_shift[:, 0:1], -float(I), ALU.mult, ALU.mult)
         w = sb.tile([P, I], F32, name="w")
         nc.scalar.activation(out=w[:], in_=p[:], func=ACT.Copy, scale=inv_z[:])
 
         pc = sb.tile([P, I], F32, name="pc")
         pc_sum = sb.tile([P, 1], F32, name="pc_sum")
         nc.vector.scalar_tensor_tensor(pc[:], c0[:], gain[:], p[:], ALU.mult, ALU.mult, accum_out=pc_sum[:])
+        inv_var_z = sb.tile([P, 1], F32, name="inv_var_z")
+        nc.vector.tensor_scalar(inv_var_z[:], inv_z[:], inv_sd[:], inv_sd[:], ALU.mult, ALU.mult)
+        direct_z = sb.tile([P, I], F32, name="direct_z")
+        nc.vector.scalar_tensor_tensor(direct_z[:], w[:], pc_sum[:], pc[:], ALU.mult, ALU.subtract)
         direct = sb.tile([P, I], F32, name="direct")
-        nc.vector.scalar_tensor_tensor(direct[:], w[:], pc_sum[:], pc[:], ALU.mult, ALU.subtract)
+        nc.scalar.activation(out=direct[:], in_=direct_z[:], func=ACT.Copy, scale=inv_z[:])
         terms = sb.tile([P, I], F32, name="terms")
         through_sd = sb.tile([P, 1], F32, name="through_sd")
-        nc.vector.scalar_tensor_tensor(terms[:], direct[:], inv_var[:], neg_ce[:], ALU.mult, ALU.mult, accum_out=through_sd[:])
+        nc.vector.scalar_tensor_tensor(terms[:], direct_z[:], inv_var_z[:], ce[:], ALU.mult, ALU.mult, accum_out=through_sd[:])
         indirect_part = sb.tile([P, I], F32, name="indirect_part")
-        nc.vector.tensor_scalar(indirect_part[:], neg_ce[:], through_sd[:], -1.0 / I, ALU.mult, ALU.mult)
+        nc.vector.tensor_scalar(indirect_part[:], ce[:], through_sd[:], -1.0 / I, ALU.mult, ALU.mult)
         nc.vector.tensor_tensor(placed[:].indirect(offsets[:]), direct[:], indirect_part[:], ALU.add)
 
         start = 0

from contextlib import ExitStack

import concourse.mybir as mybir

D, E, T, I, Q = 512, 512, 2048, 512, 128
FLOPS = 2 * D * Q * I + 2 * E * Q * I

F32 = mybir.dt.float32
BF16 = mybir.dt.bfloat16
I32 = mybir.dt.int32
U32 = mybir.dt.uint32
U16 = mybir.dt.uint16
U8 = mybir.dt.uint8
FP8X4 = mybir.dt.float8_e4m3fn_x4
ALU = mybir.AluOpType
ACT = mybir.ActivationFunctionType

P = 128
PACK = 4
EPS = 0.05
VALS_PLANE = 4
STORE_COLS = [256, 384, 384, 384, 384, 256]


def load_scale_rows(queue, plane, scales, first):
    for row in range(4):
        queue.dma_start(
            out=plane[first + row : P : 32, :].bitcast(I32),
            in_=scales[0, row:16:4, :].bitcast(I32),
        )


def load_words(queue, tile, words):
    queue.dma_start(out=tile[:].bitcast(I32), in_=words[0].rearrange("p n t -> p (n t)").bitcast(I32))


def tile_attend_bstandardised_s_kernel(tc, query, keys_words, keys_scales, sharp, gout, vals_words, vals_scales, old, offs, out):
    nc = tc.nc
    with ExitStack() as ctx:
        sb = ctx.enter_context(tc.tile_pool(name="sb", bufs=1))
        shared = ctx.enter_context(tc.tile_pool(name="shared", bufs=1))
        ps = ctx.enter_context(tc.psum_pool(name="ps", bufs=1))

        offsets = sb.tile([P, I // 16], U16, name="offsets")
        q_raw = sb.tile([P, PACK, Q], F32, name="q_raw")
        g_raw = shared.tile([P, PACK, Q], F32, name="g_raw", align_bytes=64, offset=9 * T)
        k_pool = shared.tile([P, T], U32, name="k_pool", align_bytes=64, offset=0)
        v_pool = shared.tile([P, T], U32, name="v_pool", align_bytes=64, offset=4 * T)
        ks_pool = sb.tile([P, T], U8, name="ks_pool", align_bytes=64)
        vs_pool = sb.tile([P, T], U8, name="vs_pool", align_bytes=64)
        old_sb = sb.tile([P, T], F32, name="old_sb")
        placed = sb.tile([P, T], F32, name="placed")
        sharp_sb = sb.tile([P, 1], F32, name="sharp_sb")
        sharp_up = sb.tile([P, 1], F32, name="sharp_up")
        sharp_down = sb.tile([P, 1], F32, name="sharp_down")
        minus_half = sb.tile([P, 1], F32, name="minus_half")

        nc.vector.memset(ks_pool[:, 0 : T // 2].bitcast(I32), 0)
        nc.gpsimd.memset(ks_pool[:, T // 2 : T].bitcast(I32), 0)
        nc.gpsimd.dma_start(out=sharp_sb[:], in_=sharp)
        nc.vector.memset(vs_pool[:].bitcast(I32), 0)
        nc.vector.memset(placed[:], 0.0)
        nc.gpsimd.memset(minus_half[:], -0.5)

        nc.sync.dma_start(offsets[:], offs)
        nc.sync.dma_start(out=q_raw[:], in_=query.rearrange("(p j) w -> p j w", j=PACK))
        load_scale_rows(nc.sync, ks_pool, keys_scales, 0)
        load_words(nc.sync, k_pool, keys_words)
        load_scale_rows(nc.sync, vs_pool, vals_scales, VALS_PLANE)
        nc.sync.dma_start(out=g_raw[:], in_=gout.rearrange("(p j) w -> p j w", j=PACK))
        load_words(nc.sync, v_pool, vals_words)
        nc.sync.dma_start(out=old_sb[:], in_=old)

        def round_and_interleave(raw, name):
            grouped = sb.tile([P, Q, PACK], BF16, name=name, align_bytes=64)
            nc.scalar.activation(out=grouped[:], in_=raw[:].rearrange("p j w -> p w j"), func=ACT.Copy)
            return grouped

        def quantise(grouped, codes, name):
            plane = sb.tile([P, Q], U8, name=name + "_plane", align_bytes=64)
            nc.vector.quantize_mx(out=codes[:].bitcast(FP8X4), scales=plane[:], in_=grouped[:].rearrange("p w j -> p (w j)"))
            return plane

        def gather(picked, pool_tile):
            nc.vector.tensor_copy(picked[:], pool_tile[:].indirect(offsets[:]))

        q_grouped = round_and_interleave(q_raw, "q_grouped")
        nc.gpsimd.tensor_scalar(sharp_up[:], sharp_sb[:], float(I), 1.0, ALU.mult, ALU.mult)
        nc.gpsimd.tensor_scalar(sharp_down[:], sharp_sb[:], -float(I), 1.0, ALU.mult, ALU.mult)
        g_grouped = round_and_interleave(g_raw, "g_grouped")
        ks = sb.tile([P, I], U8, name="ks", align_bytes=64)
        gather(ks, ks_pool)
        q_codes = sb.tile([P, Q], U32, name="q_codes", align_bytes=64)
        q_plane = quantise(q_grouped, q_codes, "q")
        kw = sb.tile([P, I], U32, name="kw", align_bytes=64)
        a = [ps.tile([P, I // 2], F32, name="a%d" % half) for half in range(2)]
        for half in range(2):
            slots = slice(half * I // 2, (half + 1) * I // 2)
            nc.vector.tensor_copy(kw[:, slots], k_pool[:].indirect(offsets[:, half * I // 32 : (half + 1) * I // 32]))
            nc.tensor.matmul_mx(out=a[half][:], lhsT=q_codes[:].bitcast(FP8X4), lhsT_scale=q_plane[:], rhs=kw[:, slots].bitcast(FP8X4), rhs_scale=ks[:, slots], start=True, stop=True)
        vs = shared.tile([P, I], U8, name="vs", align_bytes=64, offset=0)
        gather(vs, vs_pool)

        g_codes = shared.tile([P, Q], U32, name="g_codes", align_bytes=64, offset=T)
        g_plane = quantise(g_grouped, g_codes, "g")

        scores = shared.tile([P, I], F32, name="scores", align_bytes=64, offset=9 * T)
        half_means = sb.tile([P, 2], F32, name="half_means")
        neg_mean = sb.tile([P, 1], F32, name="neg_mean")
        squares = sb.tile([P, I], F32, name="squares")
        square_sum = shared.tile([P, 1], F32, name="square_sum", align_bytes=64, offset=8 * T)
        spread2 = sb.tile([P, 1], F32, name="spread2")
        inv_sd = sb.tile([P, 1], F32, name="inv_sd")
        for half in range(2):
            slots = slice(half * I // 2, (half + 1) * I // 2)
            nc.scalar.activation(out=scores[:, slots], in_=a[half][:], func=ACT.Copy, scale=-1.0 / I, accum_out=half_means[:, half : half + 1])
        nc.scalar.activation(out=neg_mean[:], in_=half_means[:, 0:1], func=ACT.Identity, bias=half_means[:, 1:2])
        nc.scalar.activation(out=squares[:], in_=scores[:], func=ACT.Square, scale=-float(I), bias=neg_mean[:], accum_out=square_sum[:])
        nc.scalar.activation(out=spread2[:], in_=square_sum[:], func=ACT.Copy, scale=1.0 / I, bias=EPS)
        nc.gpsimd.tensor_tensor(inv_sd[:], spread2[:], minus_half[:], ALU.pow)
        signed = sb.tile([P, I], F32, name="signed")
        neg_top = sb.tile([P, 1], F32, name="neg_top")
        nc.vector.tensor_scalar(signed[:], scores[:], sharp_up[:], None, ALU.mult, ALU.min, accum_out=neg_top[:])
        below_top = shared.tile([P, I], F32, name="below_top", align_bytes=64, offset=8 * T)
        nc.scalar.activation(out=below_top[:], in_=signed[:], func=ACT.Identity, scale=-1.0, bias=neg_top[:])

        vw = sb.tile([P, I], U32, name="vw", align_bytes=64)
        c0 = ps.tile([P, I], F32, name="c0")
        for half in range(2):
            slots = slice(half * I // 2, (half + 1) * I // 2)
            nc.vector.tensor_copy(vw[:, slots], v_pool[:].indirect(offsets[:, half * I // 32 : (half + 1) * I // 32]))
            nc.tensor.matmul_mx(out=c0[:, slots], lhsT=g_codes[:].bitcast(FP8X4), lhsT_scale=g_plane[:], rhs=vw[:, slots].bitcast(FP8X4), rhs_scale=vs[VALS_PLANE:P, slots], start=True, stop=True)

        ce = shared.tile([P, I], F32, name="ce", align_bytes=64, offset=5 * T)
        nc.vector.tensor_scalar(ce[:], scores[:], -float(I), neg_mean[:], ALU.mult, ALU.add)
        gain = shared.tile([P, 1], F32, name="gain", align_bytes=64, offset=6 * T)
        nc.vector.tensor_tensor(gain[:], sharp_down[:], inv_sd[:], ALU.mult)
        p = sb.tile([P, I], F32, name="p")
        z = sb.tile([P, 1], F32, name="z")
        nc.scalar.activation(out=p[:], in_=below_top[:], func=ACT.Exp, scale=inv_sd[:], accum_out=z[:])

        inv_z = shared.tile([P, 1], F32, name="inv_z", align_bytes=64, offset=4 * T)
        nc.vector.reciprocal(inv_z[:], z[:])
        w = sb.tile([P, I], F32, name="w")
        nc.scalar.activation(out=w[:], in_=p[:], func=ACT.Copy, scale=inv_z[:])

        pc = sb.tile([P, I], F32, name="pc")
        pc_sum = sb.tile([P, 1], F32, name="pc_sum")
        nc.vector.scalar_tensor_tensor(pc[:], c0[:], gain[:], p[:], ALU.mult, ALU.mult, accum_out=pc_sum[:])
        inv_var_z = sb.tile([P, 1], F32, name="inv_var_z")
        nc.vector.tensor_scalar(inv_var_z[:], inv_z[:], inv_sd[:], inv_sd[:], ALU.mult, ALU.mult)
        direct_z = sb.tile([P, I], F32, name="direct_z")
        nc.vector.scalar_tensor_tensor(direct_z[:], w[:], pc_sum[:], pc[:], ALU.mult, ALU.subtract)
        direct = sb.tile([P, I], F32, name="direct")
        nc.scalar.activation(out=direct[:], in_=direct_z[:], func=ACT.Copy, scale=inv_z[:])
        terms = sb.tile([P, I], F32, name="terms")
        through_sd = sb.tile([P, 1], F32, name="through_sd")
        nc.vector.scalar_tensor_tensor(terms[:], direct_z[:], inv_var_z[:], ce[:], ALU.mult, ALU.mult, accum_out=through_sd[:])
        indirect_part = sb.tile([P, I], F32, name="indirect_part")
        nc.vector.tensor_scalar(indirect_part[:], ce[:], through_sd[:], -1.0 / I, ALU.mult, ALU.mult)
        nc.vector.tensor_tensor(placed[:].indirect(offsets[:]), direct[:], indirect_part[:], ALU.add)

        start = 0
        for n, width in enumerate(STORE_COLS):
            cols = slice(start, start + width)
            total = sb.tile([P, width], F32, name="total%d" % n)
            nc.vector.tensor_tensor(total[:], placed[:, cols], old_sb[:, cols], ALU.add)
            queue = nc.sync if n % 2 == 0 else nc.scalar
            queue.dma_start(out=out[:, cols], in_=total[:])
            start = start + width
